import numpy as np
import ml_dtypes

BF16 = ml_dtypes.bfloat16


def bf(x):
    return np.asarray(x, np.float32).astype(BF16)


def f32(x):
    return np.asarray(x, np.float32)


def f64(x):
    return np.asarray(x).astype(np.float64)


def striped(idx):
    return np.tile(idx.reshape(-1, 16).T, (8, 1))


S, K, M, N = 2048, 256, 128, 2048


def setup_inputs():
    return {"table": bf(np.random.standard_normal((K, S))), "w": bf(np.random.standard_normal((K, M)) / np.sqrt(K)), "r": f32(np.random.standard_normal((M, N))), "offs": striped(np.random.permutation(S))}


def reference(table, w, r, offs):
    idx = offs[:16].T.reshape(-1)
    x = f64(table)[:, idx]
    y = f64(w).T @ x
    return y + f64(r)

@@ -1,0 +1,48 @@
+import concourse.mybir as mybir
+
+BF16, F32, U16 = mybir.dt.bfloat16, mybir.dt.float32, mybir.dt.uint16
+ADD = mybir.AluOpType.add
+
+P = 128
+K, S, M, N = 256, 2048, 128, 2048
+BLOCKS = K // P
+PIECE = 512
+PIECES = N // PIECE
+COLS = PIECE // 16
+
+FLOPS = 2 * K * M * N
+
+
+def tile_gather_matmul_kernel(tc, table, w, r, offs, out):
+    nc = tc.nc
+    with (
+        tc.tile_pool(name="held", bufs=1) as held,
+        tc.psum_pool(name="psum", bufs=1) as psum,
+    ):
+        offsets = held.tile([P, N // 16], U16, name="offsets")
+        nc.sync.dma_start(offsets[:], offs)
+
+        windows = [held.tile([P, S], BF16, name=f"window{b}") for b in range(BLOCKS)]
+        weights = [held.tile([P, M], BF16, name=f"weights{b}") for b in range(BLOCKS)]
+        for b in range(BLOCKS):
+            nc.scalar.dma_start(weights[b][:], w[b * P : (b + 1) * P, :])
+            nc.sync.dma_start(windows[b][:], table[b * P : (b + 1) * P, :])
+
+        residual = held.tile([P, N], F32, name="residual")
+        nc.scalar.dma_start(residual[:], r)
+
+        result = held.tile([P, N], F32, name="result")
+        for i in range(PIECES):
+            bank = psum.tile([P, PIECE], F32, name=f"bank{i}")
+            piece = offsets[:, i * COLS : (i + 1) * COLS]
+            for b in range(BLOCKS):
+                nc.tensor.matmul(
+                    bank[:],
+                    weights[b][:],
+                    windows[b][:].indirect(piece),
+                    start=(b == 0),
+                    stop=(b == BLOCKS - 1),
+                )
+            columns = slice(i * PIECE, (i + 1) * PIECE)
+            nc.vector.tensor_tensor(result[:, columns], bank[:], residual[:, columns], ADD)
+            nc.sync.dma_start(out[:, columns], result[:, columns])

@@ -9,40 +9,45 @@ BLOCKS = K // P
 PIECE = 512
 PIECES = N // PIECE
 COLS = PIECE // 16
+HALF = S // 2
 
 FLOPS = 2 * K * M * N
 
 
 def tile_gather_matmul_kernel(tc, table, w, r, offs, out):
     nc = tc.nc
+    queues = (nc.sync, nc.scalar)
     with (
         tc.tile_pool(name="held", bufs=1) as held,
         tc.psum_pool(name="psum", bufs=1) as psum,
     ):
         offsets = held.tile([P, N // 16], U16, name="offsets")
         nc.sync.dma_start(offsets[:], offs)
+        weights = held.tile([P, BLOCKS, M], BF16, name="weights")
+        nc.scalar.dma_start(weights[:], w.rearrange("(b p) m -> p b m", p=P))
 
         windows = [held.tile([P, S], BF16, name=f"window{b}") for b in range(BLOCKS)]
-        weights = [held.tile([P, M], BF16, name=f"weights{b}") for b in range(BLOCKS)]
         for b in range(BLOCKS):
-            nc.scalar.dma_start(weights[b][:], w[b * P : (b + 1) * P, :])
-            nc.sync.dma_start(windows[b][:], table[b * P : (b + 1) * P, :])
+            for h, queue in enumerate(queues):
+                columns = slice(h * HALF, (h + 1) * HALF)
+                queue.dma_start(windows[b][:, columns], table[b * P : (b + 1) * P, columns])
 
-        residual = held.tile([P, N], F32, name="residual")
-        nc.scalar.dma_start(residual[:], r)
-
-        result = held.tile([P, N], F32, name="result")
+        residuals = [held.tile([P, PIECE], F32, name=f"residual{i}") for i in range(PIECES)]
         for i in range(PIECES):
-            bank = psum.tile([P, PIECE], F32, name=f"bank{i}")
-            piece = offsets[:, i * COLS : (i + 1) * COLS]
-            for b in range(BLOCKS):
+            queues[i % 2].dma_start(residuals[i][:], r[:, i * PIECE : (i + 1) * PIECE])
+
+        banks = [psum.tile([P, PIECE], F32, name=f"bank{i}") for i in range(PIECES)]
+        for b in range(BLOCKS):
+            for i in range(PIECES):
                 nc.tensor.matmul(
-                    bank[:],
-                    weights[b][:],
-                    windows[b][:].indirect(piece),
+                    banks[i][:],
+                    weights[:, b, :],
+                    windows[b][:].indirect(offsets[:, i * COLS : (i + 1) * COLS]),
                     start=(b == 0),
                     stop=(b == BLOCKS - 1),
                 )
-            columns = slice(i * PIECE, (i + 1) * PIECE)
-            nc.vector.tensor_tensor(result[:, columns], bank[:], residual[:, columns], ADD)
-            nc.sync.dma_start(out[:, columns], result[:, columns])
+
+        for i in range(PIECES):
+            result = held.tile([P, PIECE], F32, name=f"result{i}")
+            nc.vector.tensor_tensor(result[:], banks[i][:], residuals[i][:], ADD)
+            queues[i % 2].dma_start(out[:, i * PIECE : (i + 1) * PIECE], result[:])

@@ -10,6 +10,7 @@ PIECE = 512
 PIECES = N // PIECE
 COLS = PIECE // 16
 HALF = S // 2
+WARMUPS = 5
 
 FLOPS = 2 * K * M * N
 
@@ -35,6 +36,13 @@ def tile_gather_matmul_kernel(tc, table, w, r, offs, out):
         residuals = [held.tile([P, PIECE], F32, name=f"residual{i}") for i in range(PIECES)]
         for i in range(PIECES):
             queues[i % 2].dma_start(residuals[i][:], r[:, i * PIECE : (i + 1) * PIECE])
+
+        zeros_f32 = held.tile([P, PIECE // 2], F32, name="zeros_f32")
+        nc.vector.memset(zeros_f32[:], 0.0)
+        zeros = zeros_f32[:].bitcast(BF16)
+        unread = psum.tile([P, PIECE], F32, name="unread")
+        for turn in range(WARMUPS):
+            nc.tensor.matmul(unread[:], zeros[:, :M], zeros, start=True, stop=True)
 
         banks = [psum.tile([P, PIECE], F32, name=f"bank{i}") for i in range(PIECES)]
         for b in range(BLOCKS):

@@ -6,11 +6,11 @@ ADD = mybir.AluOpType.add
 P = 128
 K, S, M, N = 256, 2048, 128, 2048
 BLOCKS = K // P
-PIECE = 512
-PIECES = N // PIECE
-COLS = PIECE // 16
+BANK = 512
+WIDTHS = (BANK, BANK, BANK, BANK // 2, BANK // 2)
+STARTS = tuple(sum(WIDTHS[:i]) for i in range(len(WIDTHS)))
+assert sum(WIDTHS) == N
 HALF = S // 2
-WARMUPS = 5
 
 FLOPS = 2 * K * M * N
 
@@ -18,6 +18,7 @@ FLOPS = 2 * K * M * N
 def tile_gather_matmul_kernel(tc, table, w, r, offs, out):
     nc = tc.nc
     queues = (nc.sync, nc.scalar)
+    pieces = [slice(start, start + width) for start, width in zip(STARTS, WIDTHS)]
     with (
         tc.tile_pool(name="held", bufs=1) as held,
         tc.psum_pool(name="psum", bufs=1) as psum,
@@ -33,29 +34,22 @@ def tile_gather_matmul_kernel(tc, table, w, r, offs, out):
                 columns = slice(h * HALF, (h + 1) * HALF)
                 queue.dma_start(windows[b][:, columns], table[b * P : (b + 1) * P, columns])
 
-        residuals = [held.tile([P, PIECE], F32, name=f"residual{i}") for i in range(PIECES)]
-        for i in range(PIECES):
-            queues[i % 2].dma_start(residuals[i][:], r[:, i * PIECE : (i + 1) * PIECE])
+        residuals = [held.tile([P, width], F32, name=f"residual{i}") for i, width in enumerate(WIDTHS)]
+        for i, piece in enumerate(pieces):
+            queues[i % 2].dma_start(residuals[i][:], r[:, piece])
 
-        zeros_f32 = held.tile([P, PIECE // 2], F32, name="zeros_f32")
-        nc.vector.memset(zeros_f32[:], 0.0)
-        zeros = zeros_f32[:].bitcast(BF16)
-        unread = psum.tile([P, PIECE], F32, name="unread")
-        for turn in range(WARMUPS):
-            nc.tensor.matmul(unread[:], zeros[:, :M], zeros, start=True, stop=True)
-
-        banks = [psum.tile([P, PIECE], F32, name=f"bank{i}") for i in range(PIECES)]
+        banks = [psum.tile([P, width], F32, name=f"bank{i}") for i, width in enumerate(WIDTHS)]
         for b in range(BLOCKS):
-            for i in range(PIECES):
+            for i, piece in enumerate(pieces):
                 nc.tensor.matmul(
                     banks[i][:],
                     weights[:, b, :],
-                    windows[b][:].indirect(offsets[:, i * COLS : (i + 1) * COLS]),
+                    windows[b][:].indirect(offsets[:, piece.start // 16 : piece.stop // 16]),
                     start=(b == 0),
                     stop=(b == BLOCKS - 1),
                 )
 
-        for i in range(PIECES):
-            result = held.tile([P, PIECE], F32, name=f"result{i}")
+        for i, piece in enumerate(pieces):
+            result = held.tile([P, WIDTHS[i]], F32, name=f"result{i}")
             nc.vector.tensor_tensor(result[:], banks[i][:], residuals[i][:], ADD)
-            queues[i % 2].dma_start(out[:, i * PIECE : (i + 1) * PIECE], result[:])
+            queues[i % 2].dma_start(out[:, piece], result[:])

@@ -10,7 +10,7 @@ BANK = 512
 WIDTHS = (BANK, BANK, BANK, BANK // 2, BANK // 2)
 STARTS = tuple(sum(WIDTHS[:i]) for i in range(len(WIDTHS)))
 assert sum(WIDTHS) == N
-HALF = S // 2
+LEAD = 3
 
 FLOPS = 2 * K * M * N
 
@@ -26,28 +26,28 @@ def tile_gather_matmul_kernel(tc, table, w, r, offs, out):
         offsets = held.tile([P, N // 16], U16, name="offsets")
         nc.sync.dma_start(offsets[:], offs)
         weights = held.tile([P, BLOCKS, M], BF16, name="weights")
-        nc.scalar.dma_start(weights[:], w.rearrange("(b p) m -> p b m", p=P))
+        nc.sync.dma_start(weights[:], w.rearrange("(b p) m -> p b m", p=P))
 
         windows = [held.tile([P, S], BF16, name=f"window{b}") for b in range(BLOCKS)]
         for b in range(BLOCKS):
-            for h, queue in enumerate(queues):
-                columns = slice(h * HALF, (h + 1) * HALF)
-                queue.dma_start(windows[b][:, columns], table[b * P : (b + 1) * P, columns])
+            nc.sync.dma_start(windows[b][:], table[b * P : (b + 1) * P, :])
 
         residuals = [held.tile([P, width], F32, name=f"residual{i}") for i, width in enumerate(WIDTHS)]
         for i, piece in enumerate(pieces):
-            queues[i % 2].dma_start(residuals[i][:], r[:, piece])
+            nc.sync.dma_start(residuals[i][:], r[:, piece])
 
         banks = [psum.tile([P, width], F32, name=f"bank{i}") for i, width in enumerate(WIDTHS)]
-        for b in range(BLOCKS):
-            for i, piece in enumerate(pieces):
-                nc.tensor.matmul(
-                    banks[i][:],
-                    weights[:, b, :],
-                    windows[b][:].indirect(offsets[:, piece.start // 16 : piece.stop // 16]),
-                    start=(b == 0),
-                    stop=(b == BLOCKS - 1),
-                )
+        order = [(b, i) for b in range(BLOCKS) for i in range(LEAD)]
+        order += [(b, i) for i in range(LEAD, len(WIDTHS)) for b in range(BLOCKS)]
+        for b, i in order:
+            piece = pieces[i]
+            nc.tensor.matmul(
+                banks[i][:],
+                weights[:, b, :],
+                windows[b][:].indirect(offsets[:, piece.start // 16 : piece.stop // 16]),
+                start=(b == 0),
+                stop=(b == BLOCKS - 1),
+            )
 
         for i, piece in enumerate(pieces):
             result = held.tile([P, WIDTHS[i]], F32, name=f"result{i}")

@@ -10,7 +10,7 @@ BANK = 512
 WIDTHS = (BANK, BANK, BANK, BANK // 2, BANK // 2)
 STARTS = tuple(sum(WIDTHS[:i]) for i in range(len(WIDTHS)))
 assert sum(WIDTHS) == N
-LEAD = 3
+RING = 3
 
 FLOPS = 2 * K * M * N
 
@@ -21,7 +21,7 @@ def tile_gather_matmul_kernel(tc, table, w, r, offs, out):
     pieces = [slice(start, start + width) for start, width in zip(STARTS, WIDTHS)]
     with (
         tc.tile_pool(name="held", bufs=1) as held,
-        tc.psum_pool(name="psum", bufs=1) as psum,
+        tc.psum_pool(name="psum", bufs=RING) as psum,
     ):
         offsets = held.tile([P, N // 16], U16, name="offsets")
         nc.sync.dma_start(offsets[:], offs)
@@ -36,20 +36,16 @@ def tile_gather_matmul_kernel(tc, table, w, r, offs, out):
         for i, piece in enumerate(pieces):
             nc.sync.dma_start(residuals[i][:], r[:, piece])
 
-        banks = [psum.tile([P, width], F32, name=f"bank{i}") for i, width in enumerate(WIDTHS)]
-        order = [(b, i) for b in range(BLOCKS) for i in range(LEAD)]
-        order += [(b, i) for i in range(LEAD, len(WIDTHS)) for b in range(BLOCKS)]
-        for b, i in order:
-            piece = pieces[i]
-            nc.tensor.matmul(
-                banks[i][:],
-                weights[:, b, :],
-                windows[b][:].indirect(offsets[:, piece.start // 16 : piece.stop // 16]),
-                start=(b == 0),
-                stop=(b == BLOCKS - 1),
-            )
-
         for i, piece in enumerate(pieces):
+            bank = psum.tile([P, WIDTHS[i]], F32, name="bank", tag="bank")
+            for b in range(BLOCKS):
+                nc.tensor.matmul(
+                    bank[:],
+                    weights[:, b, :],
+                    windows[b][:].indirect(offsets[:, piece.start // 16 : piece.stop // 16]),
+                    start=(b == 0),
+                    stop=(b == BLOCKS - 1),
+                )
             result = held.tile([P, WIDTHS[i]], F32, name=f"result{i}")
-            nc.vector.tensor_tensor(result[:], banks[i][:], residuals[i][:], ADD)
+            nc.vector.tensor_tensor(result[:], bank[:], residuals[i][:], ADD)
             queues[i % 2].dma_start(out[:, piece], result[:])

@@ -25,12 +25,13 @@ def tile_gather_matmul_kernel(tc, table, w, r, offs, out):
     ):
         offsets = held.tile([P, N // 16], U16, name="offsets")
         nc.sync.dma_start(offsets[:], offs)
-        weights = held.tile([P, BLOCKS, M], BF16, name="weights")
-        nc.sync.dma_start(weights[:], w.rearrange("(b p) m -> p b m", p=P))
 
+        weights = [held.tile([P, M], BF16, name=f"weights{b}") for b in range(BLOCKS)]
         windows = [held.tile([P, S], BF16, name=f"window{b}") for b in range(BLOCKS)]
         for b in range(BLOCKS):
-            nc.sync.dma_start(windows[b][:], table[b * P : (b + 1) * P, :])
+            features = slice(b * P, (b + 1) * P)
+            nc.sync.dma_start(weights[b][:], w[features, :])
+            nc.sync.dma_start(windows[b][:], table[features, :])
 
         residuals = [held.tile([P, width], F32, name=f"residual{i}") for i, width in enumerate(WIDTHS)]
         for i, piece in enumerate(pieces):
@@ -41,7 +42,7 @@ def tile_gather_matmul_kernel(tc, table, w, r, offs, out):
             for b in range(BLOCKS):
                 nc.tensor.matmul(
                     bank[:],
-                    weights[:, b, :],
+                    weights[b][:],
                     windows[b][:].indirect(offsets[:, piece.start // 16 : piece.stop // 16]),
                     start=(b == 0),
                     stop=(b == BLOCKS - 1),

@@ -17,7 +17,6 @@ FLOPS = 2 * K * M * N
 
 def tile_gather_matmul_kernel(tc, table, w, r, offs, out):
     nc = tc.nc
-    queues = (nc.sync, nc.scalar)
     pieces = [slice(start, start + width) for start, width in zip(STARTS, WIDTHS)]
     with (
         tc.tile_pool(name="held", bufs=1) as held,
@@ -49,4 +48,4 @@ def tile_gather_matmul_kernel(tc, table, w, r, offs, out):
                 )
             result = held.tile([P, WIDTHS[i]], F32, name=f"result{i}")
             nc.vector.tensor_tensor(result[:], bank[:], residuals[i][:], ADD)
-            queues[i % 2].dma_start(out[:, piece], result[:])
+            nc.sync.dma_start(out[:, piece], result[:])

@@ -7,7 +7,7 @@ P = 128
 K, S, M, N = 256, 2048, 128, 2048
 BLOCKS = K // P
 BANK = 512
-WIDTHS = (BANK, BANK, BANK, BANK // 2, BANK // 2)
+WIDTHS = (3 * BANK // 4, BANK, BANK, 3 * BANK // 4, BANK // 2)
 STARTS = tuple(sum(WIDTHS[:i]) for i in range(len(WIDTHS)))
 assert sum(WIDTHS) == N
 RING = 3

@@ -23,14 +23,14 @@ def tile_gather_matmul_kernel(tc, table, w, r, offs, out):
         tc.psum_pool(name="psum", bufs=RING) as psum,
     ):
         offsets = held.tile([P, N // 16], U16, name="offsets")
-        nc.sync.dma_start(offsets[:], offs)
-
         weights = [held.tile([P, M], BF16, name=f"weights{b}") for b in range(BLOCKS)]
         windows = [held.tile([P, S], BF16, name=f"window{b}") for b in range(BLOCKS)]
+        features = [slice(b * P, (b + 1) * P) for b in range(BLOCKS)]
+        nc.sync.dma_start(windows[0][:], table[features[0], :])
+        nc.sync.dma_start(offsets[:], offs)
         for b in range(BLOCKS):
-            features = slice(b * P, (b + 1) * P)
-            nc.sync.dma_start(weights[b][:], w[features, :])
-            nc.sync.dma_start(windows[b][:], table[features, :])
+            nc.sync.dma_start(weights[b][:], w[features[b], :])
+        nc.sync.dma_start(windows[1][:], table[features[1], :])
 
         residuals = [held.tile([P, width], F32, name=f"residual{i}") for i, width in enumerate(WIDTHS)]
         for i, piece in enumerate(pieces):

@@ -29,7 +29,7 @@ def tile_gather_matmul_kernel(tc, table, w, r, offs, out):
         nc.sync.dma_start(windows[0][:], table[features[0], :])
         nc.sync.dma_start(offsets[:], offs)
         for b in range(BLOCKS):
-            nc.sync.dma_start(weights[b][:], w[features[b], :])
+            nc.scalar.dma_start(weights[b][:], w[features[b], :])
         nc.sync.dma_start(windows[1][:], table[features[1], :])
 
         residuals = [held.tile([P, width], F32, name=f"residual{i}") for i, width in enumerate(WIDTHS)]

@@ -26,15 +26,14 @@ def tile_gather_matmul_kernel(tc, table, w, r, offs, out):
         weights = [held.tile([P, M], BF16, name=f"weights{b}") for b in range(BLOCKS)]
         windows = [held.tile([P, S], BF16, name=f"window{b}") for b in range(BLOCKS)]
         features = [slice(b * P, (b + 1) * P) for b in range(BLOCKS)]
-        nc.sync.dma_start(windows[0][:], table[features[0], :])
         nc.sync.dma_start(offsets[:], offs)
         for b in range(BLOCKS):
-            nc.scalar.dma_start(weights[b][:], w[features[b], :])
-        nc.sync.dma_start(windows[1][:], table[features[1], :])
+            nc.sync.dma_start(weights[b][:], w[features[b], :])
+            nc.scalar.dma_start(windows[b][:], table[features[b], :])
 
         residuals = [held.tile([P, width], F32, name=f"residual{i}") for i, width in enumerate(WIDTHS)]
         for i, piece in enumerate(pieces):
-            nc.sync.dma_start(residuals[i][:], r[:, piece])
+            nc.scalar.dma_start(residuals[i][:], r[:, piece])
 
         for i, piece in enumerate(pieces):
             bank = psum.tile([P, WIDTHS[i]], F32, name="bank", tag="bank")

@@ -11,6 +11,8 @@ WIDTHS = (3 * BANK // 4, BANK, BANK, 3 * BANK // 4, BANK // 2)
 STARTS = tuple(sum(WIDTHS[:i]) for i in range(len(WIDTHS)))
 assert sum(WIDTHS) == N
 RING = 3
+REGION = 56 * 1024
+SMALL = S * 2
 
 FLOPS = 2 * K * M * N
 
@@ -22,16 +24,22 @@ def tile_gather_matmul_kernel(tc, table, w, r, offs, out):
         tc.tile_pool(name="held", bufs=1) as held,
         tc.psum_pool(name="psum", bufs=RING) as psum,
     ):
-        offsets = held.tile([P, N // 16], U16, name="offsets")
-        weights = [held.tile([P, M], BF16, name=f"weights{b}") for b in range(BLOCKS)]
-        windows = [held.tile([P, S], BF16, name=f"window{b}") for b in range(BLOCKS)]
+        offsets = held.tile([P, N // 16], U16, name="offsets", offset=SMALL)
+        weights = [
+            held.tile([P, M], BF16, name=f"weights{b}", offset=SMALL + (N // 16 + b * M) * 2)
+            for b in range(BLOCKS)
+        ]
+        windows = [held.tile([P, S], BF16, name=f"window{b}", offset=b * REGION) for b in range(BLOCKS)]
         features = [slice(b * P, (b + 1) * P) for b in range(BLOCKS)]
         nc.sync.dma_start(offsets[:], offs)
         for b in range(BLOCKS):
             nc.sync.dma_start(weights[b][:], w[features[b], :])
             nc.scalar.dma_start(windows[b][:], table[features[b], :])
 
-        residuals = [held.tile([P, width], F32, name=f"residual{i}") for i, width in enumerate(WIDTHS)]
+        residuals = [
+            held.tile([P, width], F32, name=f"residual{i}", offset=2 * REGION + STARTS[i] * 4)
+            for i, width in enumerate(WIDTHS)
+        ]
         for i, piece in enumerate(pieces):
             nc.scalar.dma_start(residuals[i][:], r[:, piece])
 
@@ -45,6 +53,6 @@ def tile_gather_matmul_kernel(tc, table, w, r, offs, out):
                     start=(b == 0),
                     stop=(b == BLOCKS - 1),
                 )
-            result = held.tile([P, WIDTHS[i]], F32, name=f"result{i}")
+            result = held.tile([P, WIDTHS[i]], F32, name=f"result{i}", offset=3 * REGION + STARTS[i] * 4)
             nc.vector.tensor_tensor(result[:], bank[:], residuals[i][:], ADD)
             nc.sync.dma_start(out[:, piece], result[:])

@@ -53,6 +53,5 @@ def tile_gather_matmul_kernel(tc, table, w, r, offs, out):
                     start=(b == 0),
                     stop=(b == BLOCKS - 1),
                 )
-            result = held.tile([P, WIDTHS[i]], F32, name=f"result{i}", offset=3 * REGION + STARTS[i] * 4)
-            nc.vector.tensor_tensor(result[:], bank[:], residuals[i][:], ADD)
-            nc.sync.dma_start(out[:, piece], result[:])
+            nc.vector.tensor_tensor(residuals[i][:], bank[:], residuals[i][:], ADD)
+            nc.sync.dma_start(out[:, piece], residuals[i][:])

@@ -11,8 +11,6 @@ WIDTHS = (3 * BANK // 4, BANK, BANK, 3 * BANK // 4, BANK // 2)
 STARTS = tuple(sum(WIDTHS[:i]) for i in range(len(WIDTHS)))
 assert sum(WIDTHS) == N
 RING = 3
-REGION = 56 * 1024
-SMALL = S * 2
 
 FLOPS = 2 * K * M * N
 
@@ -24,24 +22,18 @@ def tile_gather_matmul_kernel(tc, table, w, r, offs, out):
         tc.tile_pool(name="held", bufs=1) as held,
         tc.psum_pool(name="psum", bufs=RING) as psum,
     ):
-        offsets = held.tile([P, N // 16], U16, name="offsets", offset=SMALL)
-        weights = [
-            held.tile([P, M], BF16, name=f"weights{b}", offset=SMALL + (N // 16 + b * M) * 2)
-            for b in range(BLOCKS)
-        ]
-        windows = [held.tile([P, S], BF16, name=f"window{b}", offset=b * REGION) for b in range(BLOCKS)]
+        offsets = held.tile([P, N // 16], U16, name="offsets")
+        weights = [held.tile([P, M], BF16, name=f"weights{b}") for b in range(BLOCKS)]
+        windows = [held.tile([P, S], BF16, name=f"window{b}") for b in range(BLOCKS)]
         features = [slice(b * P, (b + 1) * P) for b in range(BLOCKS)]
         nc.sync.dma_start(offsets[:], offs)
         for b in range(BLOCKS):
             nc.sync.dma_start(weights[b][:], w[features[b], :])
             nc.scalar.dma_start(windows[b][:], table[features[b], :])
 
-        residuals = [
-            held.tile([P, width], F32, name=f"residual{i}", offset=2 * REGION + STARTS[i] * 4)
-            for i, width in enumerate(WIDTHS)
-        ]
+        sums = [held.tile([P, width], F32, name=f"sum{i}") for i, width in enumerate(WIDTHS)]
         for i, piece in enumerate(pieces):
-            nc.scalar.dma_start(residuals[i][:], r[:, piece])
+            nc.scalar.dma_start(sums[i][:], r[:, piece])
 
         for i, piece in enumerate(pieces):
             bank = psum.tile([P, WIDTHS[i]], F32, name="bank", tag="bank")
@@ -53,5 +45,5 @@ def tile_gather_matmul_kernel(tc, table, w, r, offs, out):
                     start=(b == 0),
                     stop=(b == BLOCKS - 1),
                 )
-            nc.vector.tensor_tensor(residuals[i][:], bank[:], residuals[i][:], ADD)
-            nc.sync.dma_start(out[:, piece], residuals[i][:])
+            nc.vector.tensor_tensor(sums[i][:], bank[:], sums[i][:], ADD)
+            nc.sync.dma_start(out[:, piece], sums[i][:])

import concourse.mybir as mybir

BF16, F32, U16 = mybir.dt.bfloat16, mybir.dt.float32, mybir.dt.uint16
ADD = mybir.AluOpType.add

P = 128
K, S, M, N = 256, 2048, 128, 2048
BLOCKS = K // P
BANK = 512
WIDTHS = (3 * BANK // 4, BANK, BANK, 3 * BANK // 4, BANK // 2)
STARTS = tuple(sum(WIDTHS[:i]) for i in range(len(WIDTHS)))
assert sum(WIDTHS) == N
RING = 3

FLOPS = 2 * K * M * N


def tile_gather_matmul_kernel(tc, table, w, r, offs, out):
    nc = tc.nc
    pieces = [slice(start, start + width) for start, width in zip(STARTS, WIDTHS)]
    with (
        tc.tile_pool(name="held", bufs=1) as held,
        tc.psum_pool(name="psum", bufs=RING) as psum,
    ):
        offsets = held.tile([P, N // 16], U16, name="offsets")
        weights = [held.tile([P, M], BF16, name=f"weights{b}") for b in range(BLOCKS)]
        windows = [held.tile([P, S], BF16, name=f"window{b}") for b in range(BLOCKS)]
        features = [slice(b * P, (b + 1) * P) for b in range(BLOCKS)]
        nc.sync.dma_start(offsets[:], offs)
        for b in range(BLOCKS):
            nc.sync.dma_start(weights[b][:], w[features[b], :])
            nc.scalar.dma_start(windows[b][:], table[features[b], :])

        sums = [held.tile([P, width], F32, name=f"sum{i}") for i, width in enumerate(WIDTHS)]
        for i, piece in enumerate(pieces):
            nc.scalar.dma_start(sums[i][:], r[:, piece])

        for i, piece in enumerate(pieces):
            bank = psum.tile([P, WIDTHS[i]], F32, name="bank", tag="bank")
            for b in range(BLOCKS):
                nc.tensor.matmul(
                    bank[:],
                    weights[b][:],
                    windows[b][:].indirect(offsets[:, piece.start // 16 : piece.stop // 16]),
                    start=(b == 0),
                    stop=(b == BLOCKS - 1),
                )
            nc.vector.tensor_tensor(sums[i][:], bank[:], sums[i][:], ADD)
            nc.sync.dma_start(out[:, piece], sums[i][:])
